import numpy as np
import ml_dtypes


def mxq(x, axis, fmt="e4m3"):
    dtype, down = {"e4m3": (ml_dtypes.float8_e4m3fn, 7), "e5m2": (ml_dtypes.float8_e5m2, 14)}[fmt]
    v = np.moveaxis(np.asarray(x, np.float32).astype(ml_dtypes.bfloat16).astype(np.float64), axis, -1)
    blocks = v.reshape(v.shape[:-1] + (-1, 32))
    amax = np.abs(blocks).max(-1, keepdims=True)
    byte = np.maximum(np.where(amax > 0, np.frexp(amax)[1] - 1 + 127, 0) - down, 1)
    scale = np.exp2(byte - 127.0)
    codes = (blocks / scale).astype(np.float32).astype(dtype).astype(np.float64)
    return np.moveaxis((codes * scale).reshape(v.shape), -1, axis)


WIDE = False


def mx_kscale(k):
    if not WIDE:
        return np.ones(k)
    levels = np.array([10, -10, 5, -5, 0])
    if k % 512:
        return np.exp2(np.random.permutation(np.resize(levels, k // 32))).repeat(32)
    a = np.empty((k // 512, 16))
    for p in range(k // 512):
        a[p, :8] = np.random.permutation(np.resize(levels, 8))
        for g in range(8):
            far = levels[np.abs(levels - a[p, g]) >= 10]
            a[p, g + 8] = far[np.random.randint(len(far))]
    return np.exp2(a.ravel()).repeat(32)


def f64(x):
    return np.asarray(x).astype(np.float64)


def striped(idx):
    return np.tile(np.asarray(idx).reshape(-1, 16).T, (8, 1)).astype(np.uint16)


def unstriped(offs):
    return offs[:16].T.reshape(-1).astype(np.int64)


E2M1 = np.array([0.0, 0.5, 1.0, 1.5, 2.0, 3.0, 4.0, 6.0, -0.0, -0.5, -1.0, -1.5, -2.0, -3.0, -4.0, -6.0])


def pack_weight(w, fmt):
    k, n = w.shape
    w = f64(np.asarray(w, np.float32).astype(ml_dtypes.bfloat16)).reshape(k // 32, 32, n)
    amax = np.abs(w).max(1)
    if fmt == "e4m3":
        byte = np.frexp(amax)[1] - 1 + 127 - 7
    else:
        mant, ex = np.frexp(amax / 6.0)
        byte = np.where(mant > 0.5, ex, ex - 1) + 127
    byte = np.clip(np.where(amax > 0, byte, 1), 1, 254)
    scaled = (w * np.exp2(127.0 - byte)[:, None, :]).reshape(k, n).astype(np.float32)
    by_word = np.ascontiguousarray(scaled.reshape(k // 512, 128, 4, n).transpose(0, 1, 3, 2))
    if fmt == "e4m3":
        words = by_word.astype(ml_dtypes.float8_e4m3fn).view(np.uint8)
    else:
        c = by_word.astype(ml_dtypes.float4_e2m1fn).view(np.uint8) & 0xF
        words = (c[..., 0::2] | (c[..., 1::2] << 4)).reshape(k // 512, 128, 2 * n)
    return np.ascontiguousarray(words), np.ascontiguousarray(byte.astype(np.uint8).reshape(k // 512, 16, n))


def unpack_weight(words, scales, fmt):
    g, _, n = scales.shape
    words = np.ascontiguousarray(words).reshape(g, 128, n, -1)
    if fmt == "e4m3":
        vals = words.view(ml_dtypes.float8_e4m3fn).astype(np.float64)
    else:
        nib = np.empty((g, 128, n, 4), np.uint8)
        nib[..., 0::2] = words & 0xF
        nib[..., 1::2] = words >> 4
        vals = E2M1[nib]
    vals = vals * np.repeat(np.exp2(scales.astype(np.float64) - 127.0), 8, axis=1)[..., None]
    return vals.transpose(0, 1, 3, 2).reshape(g * 512, n)


def bf(x):
    return np.asarray(x, np.float32).astype(ml_dtypes.bfloat16)


def planes(Y):
    r, m = Y.shape
    b = f64(bf(Y)).reshape(r // 32, 32, m)
    amax = np.abs(b).max(1)
    byte = np.clip(np.where(amax > 0, np.frexp(amax)[1] - 1 + 127 - 7, 1), 1, 254)
    codes = (b * np.exp2(127.0 - byte)[:, None, :]).reshape(r, m).astype(np.float32).astype(ml_dtypes.float8_e4m3fn).view(np.uint8)
    words = codes.reshape(r // 512, 128, 4, m).transpose(0, 1, 3, 2)
    return np.ascontiguousarray(words), np.ascontiguousarray(byte.astype(np.uint8).reshape(r // 512, 16, m))


D, T, I, J, U, Z, E, Y = 512, 2048, 512, 512, 1024, 1024, 512, 1024


def setup_inputs():
    n = np.random.standard_normal
    idx = np.random.permutation(T)[:I]
    idx2 = np.random.permutation(U)[:J]
    idx3 = np.random.permutation(Z)[:J]
    idx4 = np.random.permutation(Y)[:I]
    fd = mx_kscale(D)
    fi = mx_kscale(I)
    ti = np.ones(T)
    ti[idx] = fi
    ti4 = np.ones(Y)
    ti4[idx4] = fi
    keysp = pack_weight(n((D, T)) / fd[:, None], "e2m1")
    return {
        "keys_words": keysp[0],
        "keys_scales": keysp[1],
        "notes": (n((D, U)) * 1.0 / np.sqrt(D) * fd[:, None]).astype(np.float32),
        "given": (np.random.uniform(0.3, 1.7, (I, Z))).astype(np.float32),
        "rowf": (np.random.uniform(0.02, 0.08, (I, 1)) * fi[:, None]).astype(np.float32),
        "rowf2": (np.random.uniform(0.02, 0.08, (I, 1)) * fi[:, None]).astype(np.float32),
        "vals": (n((E, T)) / ti).astype(np.float32),
        "vals2": (n((E, Y)) / ti4).astype(np.float32),
        "offs": striped(idx),
        "offs2": striped(idx2),
        "offs3": striped(idx3),
        "offs4": striped(idx4),
    }


def reference(keys_words, keys_scales, notes, given, rowf, rowf2, vals, vals2, offs, offs2, offs3, offs4):
    idx = unstriped(offs)
    idx2 = unstriped(offs2)
    idx3 = unstriped(offs3)
    idx4 = unstriped(offs4)
    keysu = unpack_weight(keys_words, keys_scales, "e2m1")
    keysidxg = keysu[:, idx]
    notesidx2q = mxq(f64(notes)[:, idx2], 0, "e4m3")
    g1 = keysidxg.T @ notesidx2q
    g0 = g1 * f64(given)[:, idx3]
    gr1 = g0 * f64(rowf)
    gr2 = g0 * f64(rowf2)
    vt1 = f64(vals)[:, idx].T
    vt2 = f64(vals2)[:, idx4].T
    vt1q = mxq(vt1, 0, "e4m3")
    gr1q = mxq(gr1, 0, "e4m3")
    vt2q = mxq(vt2, 0, "e4m3")
    gr2q = mxq(gr2, 0, "e4m3")
    o = vt1q.T @ gr1q + vt2q.T @ gr2q
    words, scales = planes(o)
    return o, words, scales

@@ -1,0 +1,279 @@
+from contextlib import ExitStack
+
+import concourse.mybir as mybir
+from concourse.masks import make_identity
+
+D, T, I, J, U, Z, E, Y = 512, 2048, 512, 512, 1024, 1024, 512, 1024
+FLOPS = 2 * D * I * J + 2 * 2 * I * E * J
+
+F32 = mybir.dt.float32
+BF16 = mybir.dt.bfloat16
+I32 = mybir.dt.int32
+U32 = mybir.dt.uint32
+U16 = mybir.dt.uint16
+U8 = mybir.dt.uint8
+FP8X4 = mybir.dt.float8_e4m3fn_x4
+FP4X4 = mybir.dt.float4_e2m1fn_x4
+MULT = mybir.AluOpType.mult
+COPY = mybir.ActivationFunctionType.Copy
+
+P = 128
+PACK = 4
+N = 512
+HALF = N // 2
+LAST = PACK - 1
+
+
+def tile_attend_tab_timestable_twostores_pl_kernel(
+    tc, keys_words, keys_scales, notes, given, rowf, rowf2, vals, vals2, offs, offs2, offs3, offs4, out_0, out_1, out_2
+):
+    nc = tc.nc
+    with ExitStack() as ctx:
+        keep = ctx.enter_context(tc.tile_pool(name="keep", bufs=1))
+        late = ctx.enter_context(tc.tile_pool(name="late", bufs=1))
+        psum = ctx.enter_context(tc.psum_pool(name="psum", bufs=1))
+
+        def tile(name, shape, dtype, tag=None):
+            return keep.tile(shape, dtype, name=name, tag=tag or name, align_bytes=64)
+
+        def bank_tile(name, shape, bank):
+            return psum.tile(shape, F32, name=name, tag=f"bank{bank}")
+
+        def plane(src, r):
+            return src.rearrange("(p r) c -> p r c", r=PACK)[:, r, :]
+
+        def interleave(engine_copy, dst, src):
+            engine_copy(
+                dst.rearrange("p (c i) t -> p c t i", i=4),
+                src.rearrange("p t (c i) -> p c t i", i=4),
+            )
+
+        def scalar_gather(dst, window, offsets):
+            nc.scalar.activation(dst, window[:].indirect(offsets), COPY)
+
+        def vector_gather(dst, window, offsets):
+            nc.vector.tensor_copy(dst, window[:].indirect(offsets))
+
+        def split_gather(dst, window, offsets):
+            cols = HALF // 16
+            scalar_gather(dst[:, :HALF], window, offsets[:, :cols])
+            vector_gather(dst[:, HALF:], window, offsets[:, cols:])
+
+        lists = [tile(f"list{n}", [P, N // 16], U16) for n in range(4)]
+        key_words = tile("key_words", [P, T], U16)
+        key_bytes = tile("key_bytes", [P, T], U8)
+        note_win = [tile(f"note_win{t}", [P, U], F32) for t in range(PACK)]
+        given_win = [tile(f"given_win{t}", [P, Z], F32) for t in range(PACK)]
+        val_win = [tile(f"val_win{r}", [P, T], F32) for r in range(LAST)]
+        val_win.append(late.tile([P, T], F32, name="val_win_last", align_bytes=64, offset=0))
+        val2_win = [tile(f"val2_win{r}", [P, Y], F32) for r in range(LAST)]
+        val2_win.append(late.tile([P, Y], F32, name="val2_win_last", align_bytes=64, offset=8192))
+        factor = [tile(f"factor{s}", [P, PACK], F32) for s in range(2)]
+        identity = tile("identity", [P, P], F32)
+
+        nc.gpsimd.memset(key_bytes[:, : T // 2].bitcast(I32), 0)
+        nc.vector.memset(key_bytes[:, T // 2 :].bitcast(I32), 0)
+        make_identity(nc, identity[:])
+
+        def load(dst, src):
+            nc.sync.dma_start(out=dst, in_=src)
+
+        def load_key_bytes(q):
+            load(key_bytes[32 * q : 32 * q + 4, :].bitcast(I32), keys_scales[0, 4 * q : 4 * q + 4, :].bitcast(I32))
+
+        load(note_win[0][:], plane(notes, 0))
+        load(lists[1][:], offs2)
+        load(key_words[:].bitcast(I32), keys_words[0].bitcast(I32))
+        load(lists[0][:], offs)
+        for q in range(4):
+            load_key_bytes(q)
+        load(note_win[1][:], plane(notes, 1))
+        load(lists[2][:], offs3)
+        load(lists[3][:], offs4)
+        load(note_win[2][:], plane(notes, 2))
+        load(factor[0][:], rowf.rearrange("(p t) o -> p (t o)", t=PACK))
+        load(factor[1][:], rowf2.rearrange("(p t) o -> p (t o)", t=PACK))
+        load(note_win[3][:], plane(notes, 3))
+        for t in range(PACK):
+            load(given_win[t][:], plane(given, t))
+        for r in range(PACK):
+            load(val2_win[r][:], plane(vals2, r))
+            load(val_win[r][:], plane(vals, r))
+
+        note_planes = tile("note_planes", [P, PACK, N], BF16)
+        scalar_gather(note_planes[:, 0, :], note_win[0], lists[1][:])
+        scalar_gather(note_planes[:, 1, :], note_win[1], lists[1][:])
+        scalar_gather(note_planes[:, 2, :], note_win[2], lists[1][:])
+
+        picked_words = tile("picked_words", [P, N], U16)
+        dealt_words = tile("dealt_words", [P, PACK, P], U16)
+        dealt_bytes = tile("dealt_bytes", [P, PACK, P], U8)
+        vector_gather(picked_words[:], key_words, lists[0][:])
+        vector_gather(dealt_bytes[:].rearrange("p t m -> p m t"), key_bytes, lists[0][:])
+        nc.vector.tensor_copy(dealt_words[:], picked_words[:].rearrange("p (m t) -> p t m", t=PACK))
+
+        note_rows = tile("note_rows", [P, N, PACK], BF16)
+        interleave(nc.vector.tensor_copy, note_rows[:, :, 0:2], note_planes[:, 0:2, :])
+        split_gather(note_planes[:, LAST, :], note_win[LAST], lists[1])
+        note_codes = tile("note_codes", [P, N], U32)
+        note_scales = tile("note_scales", [P, N], U8)
+        interleave(nc.vector.tensor_copy, note_rows[:, :, 2:4], note_planes[:, 2:4, :])
+        nc.vector.quantize_mx(
+            out=note_codes[:].bitcast(FP8X4), scales=note_scales[:], in_=note_rows[:].rearrange("p j t -> p (j t)")
+        )
+
+        given_cols = tile("given_cols", [P, PACK, N], F32)
+        for t in range(PACK):
+            scalar_gather(given_cols[:, t, :], given_win[t], lists[2][:])
+
+        products = []
+        for t in range(PACK):
+            bank = bank_tile(f"product{t}", [P, N], t)
+            nc.tensor.matmul_mx(
+                out=bank[:],
+                lhsT=dealt_words[:, t, :].bitcast(FP4X4),
+                lhsT_scale=dealt_bytes[:, t, :],
+                rhs=note_codes[:].bitcast(FP8X4),
+                rhs_scale=note_scales[:],
+                start=True,
+                stop=True,
+            )
+            products.append(bank)
+
+        table_planes = [tile(f"table_planes{s}", [P, PACK, N], BF16) for s in range(2)]
+        table_rows = [tile(f"table_rows{s}", [P, N, PACK], BF16) for s in range(2)]
+        table_codes = [tile(f"table_codes{s}", [P, N], U32) for s in range(2)]
+        table_scales = [tile(f"table_scales{s}", [P, N], U8) for s in range(2)]
+        for t in range(PACK):
+            for s in range(2):
+                nc.vector.scalar_tensor_tensor(
+                    out=table_planes[s][:, t, :],
+                    in0=products[t][:],
+                    scalar=factor[s][:, t : t + 1],
+                    in1=given_cols[:, t, :],
+                    op0=MULT,
+                    op1=MULT,
+                )
+        for s in (1, 0):
+            interleave(nc.vector.tensor_copy, table_rows[s][:], table_planes[s][:])
+        for s in (1, 0):
+            nc.vector.quantize_mx(
+                out=table_codes[s][:].bitcast(FP8X4),
+                scales=table_scales[s][:],
+                in_=table_rows[s][:].rearrange("p j t -> p (j t)"),
+            )
+
+        value_codes = tile("value_codes", [P, 2 * PACK * P], U32, tag="table_planes0")
+        value_scales = tile("value_scales", [P, 2 * PACK * P], U8)
+
+        def pick(slot, split, tag=None):
+            r, s = slot // 2, 1 - slot % 2
+            window, offsets = (val2_win[r], lists[3]) if s == 1 else (val_win[r], lists[0])
+            picked = tile(f"picked{slot}", [P, N], BF16, tag=tag)
+            if split:
+                split_gather(picked, window, offsets)
+            else:
+                scalar_gather(picked[:], window, offsets[:])
+            return picked
+
+        def turn(picked_tiles, slot, bank, copy, rows):
+            n = len(picked_tiles)
+            turned = bank_tile(f"turned{slot}", [P, n, 2, P], bank)
+            for k, picked in enumerate(picked_tiles):
+                pairs = picked[:].bitcast(F32)
+                for u in range(2):
+                    nc.tensor.transpose(turned[:, k, u, :], pairs[:, u::2], identity[:])
+            copy(
+                rows[:].bitcast(F32).rearrange("p (k m u) -> p k m u", k=n, u=2),
+                turned[:].rearrange("p k u m -> p k m u"),
+            )
+            return rows
+
+        def quantize_values(rows, slot):
+            cols = slice(slot * P, slot * P + rows.shape[1] // PACK)
+            nc.vector.quantize_mx(out=value_codes[:, cols].bitcast(FP8X4), scales=value_scales[:, cols], in_=rows[:])
+
+        def multiply(bank, slot, cols):
+            s = 1 - slot % 2
+            own = slice(slot * P, (slot + 1) * P)
+            nc.tensor.matmul_mx(
+                out=bank,
+                lhsT=value_codes[:, own].bitcast(FP8X4),
+                lhsT_scale=value_scales[:, own],
+                rhs=table_codes[s][:, cols].bitcast(FP8X4),
+                rhs_scale=table_scales[s][:, cols],
+                start=(slot % 2 == 0),
+                stop=(slot % 2 == 1),
+            )
+
+        low = late.tile([P, 2, N], F32, name="low", align_bytes=64, offset=8192 + 2048)
+        high = late.tile([P, 2, N], F32, name="high", align_bytes=64, offset=0)
+        result_rows = late.tile([P, N, PACK], BF16, name="result_rows", align_bytes=64, offset=4096)
+        result_codes = tile("result_codes", [P, N], U32)
+        result_scales = tile("result_scales", [P, N], U8)
+        halves = [slice(0, HALF), slice(HALF, N)]
+        whole = slice(0, N)
+
+        def result(r, cols):
+            return (low, high)[r // 2][:, r % 2, cols]
+
+        def store_plane(r):
+            nc.sync.dma_start(out=plane(out_0, r), in_=result(r, whole))
+
+        sums = []
+
+        def finish(r, rows, bank):
+            sums.append(bank_tile(f"sum{r}", [P, N], bank))
+            quantize_values(rows, 2 * r)
+            for slot in (2 * r, 2 * r + 1):
+                multiply(sums[r][:], slot, whole)
+
+        def copy_out(r):
+            nc.scalar.copy(result(r, whole), sums[r][:])
+            store_plane(r)
+
+        rows01 = tile("rows01", [P, 2 * N], BF16)
+        turn([pick(0, False), pick(1, False)], 0, 4, nc.vector.tensor_copy, rows01)
+        picked23 = [pick(2, False), pick(3, False)]
+        picked4 = pick(4, False)
+        rows23 = tile("rows23", [P, 2 * N], BF16, tag="val2_win2")
+        turn(picked23, 2, 5, nc.scalar.copy, rows23)
+        finish(0, rows01, 5)
+        finish(1, rows23, 1)
+        picked5 = pick(5, True)
+        picked6 = pick(6, True)
+        rows45 = late.tile([P, 2 * N], BF16, name="rows45", align_bytes=64, offset=8192)
+        finish(2, turn([picked4, picked5], 4, 6, nc.vector.tensor_copy, rows45), 2)
+        copy_out(0)
+        rows6 = tile("rows6", [P, N], BF16)
+        quantize_values(turn([picked6], 6, 7, nc.scalar.copy, rows6), 6)
+        copy_out(1)
+        half_sums = [bank_tile(f"half_sum{h}", [P, HALF], 3 + h) for h in range(2)]
+        for h in range(2):
+            multiply(half_sums[h][:], 6, halves[h])
+        picked7 = pick(7, True)
+        copy_out(2)
+        interleave(nc.vector.tensor_copy, result_rows[:, :, 0:2], low[:])
+        rows7 = tile("rows7", [P, N], BF16)
+        quantize_values(turn([picked7], 7, 5, nc.scalar.copy, rows7), 7)
+        for h in range(2):
+            multiply(half_sums[h][:], 7, halves[h])
+        for h in range(2):
+            nc.scalar.copy(result(LAST, halves[h]), half_sums[h][:])
+        for h in range(2):
+            interleave(nc.vector.tensor_copy, result_rows[:, halves[h], 2:4], high[:, :, halves[h]])
+        for h in range(2):
+            nc.vector.quantize_mx(
+                out=result_codes[:, halves[h]].bitcast(FP8X4),
+                scales=result_scales[:, halves[h]],
+                in_=result_rows[:, halves[h], :].rearrange("p j t -> p (j t)"),
+            )
+        store_plane(LAST)
+        words_out = out_1[0].rearrange("p c r -> p (c r)").bitcast(I32)
+        for h in range(2):
+            nc.sync.dma_start(out=words_out[:, halves[h]], in_=result_codes[:, halves[h]].bitcast(I32))
+        for q in range(4):
+            nc.scalar.dma_start(
+                out=out_2[0, 4 * q : 4 * q + 4, :].bitcast(I32),
+                in_=result_scales[32 * q : 32 * q + 4, :].bitcast(I32),
+            )

@@ -64,10 +64,10 @@ def tile_attend_tab_timestable_twostores_pl_kernel(
         key_bytes = tile("key_bytes", [P, T], U8)
         note_win = [tile(f"note_win{t}", [P, U], F32) for t in range(PACK)]
         given_win = [tile(f"given_win{t}", [P, Z], F32) for t in range(PACK)]
-        val_win = [tile(f"val_win{r}", [P, T], F32) for r in range(LAST)]
-        val_win.append(late.tile([P, T], F32, name="val_win_last", align_bytes=64, offset=0))
-        val2_win = [tile(f"val2_win{r}", [P, Y], F32) for r in range(LAST)]
-        val2_win.append(late.tile([P, Y], F32, name="val2_win_last", align_bytes=64, offset=8192))
+        val_win = [tile(f"val_win{r}", [P, T], F32) for r in range(2)]
+        val_win.append(late.tile([P, T], F32, name="val_win2", align_bytes=64, offset=4 * T))
+        val_win.append(late.tile([P, T], F32, name="val_win3", align_bytes=64, offset=0))
+        val2_win = [tile(f"val2_win{r}", [P, Y], F32) for r in range(PACK)]
         factor = [tile(f"factor{s}", [P, PACK], F32) for s in range(2)]
         identity = tile("identity", [P, P], F32)
 
@@ -88,16 +88,19 @@ def tile_attend_tab_timestable_twostores_pl_kernel(
         for q in range(4):
             load_key_bytes(q)
         load(note_win[1][:], plane(notes, 1))
-        load(lists[2][:], offs3)
-        load(lists[3][:], offs4)
         load(note_win[2][:], plane(notes, 2))
+        load(note_win[3][:], plane(notes, 3))
+        load(lists[2][:], offs3)
+        load(given_win[0][:], plane(given, 0))
         load(factor[0][:], rowf.rearrange("(p t) o -> p (t o)", t=PACK))
         load(factor[1][:], rowf2.rearrange("(p t) o -> p (t o)", t=PACK))
-        load(note_win[3][:], plane(notes, 3))
-        for t in range(PACK):
-            load(given_win[t][:], plane(given, t))
+        load(given_win[1][:], plane(given, 1))
+        load(given_win[2][:], plane(given, 2))
+        load(given_win[3][:], plane(given, 3))
+        load(lists[3][:], offs4)
         for r in range(PACK):
             load(val2_win[r][:], plane(vals2, r))
+        for r in range(PACK):
             load(val_win[r][:], plane(vals, r))
 
         note_planes = tile("note_planes", [P, PACK, N], BF16)
@@ -117,10 +120,16 @@ def tile_attend_tab_timestable_twostores_pl_kernel(
         split_gather(note_planes[:, LAST, :], note_win[LAST], lists[1])
         note_codes = tile("note_codes", [P, N], U32)
         note_scales = tile("note_scales", [P, N], U8)
-        interleave(nc.vector.tensor_copy, note_rows[:, :, 2:4], note_planes[:, 2:4, :])
-        nc.vector.quantize_mx(
-            out=note_codes[:].bitcast(FP8X4), scales=note_scales[:], in_=note_rows[:].rearrange("p j t -> p (j t)")
-        )
+        halves = [slice(0, HALF), slice(HALF, N)]
+        whole = slice(0, N)
+        for h in (1, 0):
+            interleave(nc.vector.tensor_copy, note_rows[:, halves[h], 2:4], note_planes[:, 2:4, halves[h]])
+        for h in (1, 0):
+            nc.vector.quantize_mx(
+                out=note_codes[:, halves[h]].bitcast(FP8X4),
+                scales=note_scales[:, halves[h]],
+                in_=note_rows[:, halves[h], :].rearrange("p j t -> p (j t)"),
+            )
 
         given_cols = tile("given_cols", [P, PACK, N], F32)
         for t in range(PACK):
@@ -129,15 +138,16 @@ def tile_attend_tab_timestable_twostores_pl_kernel(
         products = []
         for t in range(PACK):
             bank = bank_tile(f"product{t}", [P, N], t)
-            nc.tensor.matmul_mx(
-                out=bank[:],
-                lhsT=dealt_words[:, t, :].bitcast(FP4X4),
-                lhsT_scale=dealt_bytes[:, t, :],
-                rhs=note_codes[:].bitcast(FP8X4),
-                rhs_scale=note_scales[:],
-                start=True,
-                stop=True,
-            )
+            for cols in (halves[::-1] if t == 0 else [whole]):
+                nc.tensor.matmul_mx(
+                    out=bank[:, cols],
+                    lhsT=dealt_words[:, t, :].bitcast(FP4X4),
+                    lhsT_scale=dealt_bytes[:, t, :],
+                    rhs=note_codes[:, cols].bitcast(FP8X4),
+                    rhs_scale=note_scales[:, cols],
+                    start=True,
+                    stop=True,
+                )
             products.append(bank)
 
         table_planes = [tile(f"table_planes{s}", [P, PACK, N], BF16) for s in range(2)]
@@ -163,105 +173,112 @@ def tile_attend_tab_timestable_twostores_pl_kernel(
                 in_=table_rows[s][:].rearrange("p j t -> p (j t)"),
             )
 
-        value_codes = tile("value_codes", [P, 2 * PACK * P], U32, tag="table_planes0")
+        value_codes = {}
         value_scales = tile("value_scales", [P, 2 * PACK * P], U8)
 
-        def pick(slot, split, tag=None):
-            r, s = slot // 2, 1 - slot % 2
-            window, offsets = (val2_win[r], lists[3]) if s == 1 else (val_win[r], lists[0])
-            picked = tile(f"picked{slot}", [P, N], BF16, tag=tag)
+        def pick(slot, split=False):
+            window, offsets = (val2_win[slot], lists[3]) if slot < PACK else (val_win[slot - PACK], lists[0])
+            picked = tile(f"picked{slot}", [P, N], BF16)
             if split:
                 split_gather(picked, window, offsets)
             else:
                 scalar_gather(picked[:], window, offsets[:])
             return picked
 
-        def turn(picked_tiles, slot, bank, copy, rows):
-            n = len(picked_tiles)
-            turned = bank_tile(f"turned{slot}", [P, n, 2, P], bank)
+        def turn(picked_tiles, slot, bank):
+            turned = bank_tile(f"turned{slot}", [P, len(picked_tiles), 2, P], bank)
             for k, picked in enumerate(picked_tiles):
                 pairs = picked[:].bitcast(F32)
                 for u in range(2):
                     nc.tensor.transpose(turned[:, k, u, :], pairs[:, u::2], identity[:])
+            return turned
+
+        def lay_rows(turned, copy, rows):
+            n = turned.shape[1]
             copy(
-                rows[:].bitcast(F32).rearrange("p (k m u) -> p k m u", k=n, u=2),
+                rows.bitcast(F32).rearrange("p (k m u) -> p k m u", k=n, u=2),
                 turned[:].rearrange("p k u m -> p k m u"),
             )
-            return rows
 
-        def quantize_values(rows, slot):
-            cols = slice(slot * P, slot * P + rows.shape[1] // PACK)
-            nc.vector.quantize_mx(out=value_codes[:, cols].bitcast(FP8X4), scales=value_scales[:, cols], in_=rows[:])
+        def quantize_values(rows, slot, codes):
+            n = rows.shape[1] // N
+            nc.vector.quantize_mx(
+                out=codes[:].bitcast(FP8X4), scales=value_scales[:, slot * P : (slot + n) * P], in_=rows[:]
+            )
+            for k in range(n):
+                value_codes.setdefault(slot + k, codes[:, k * P : (k + 1) * P])
 
         def multiply(bank, slot, cols):
-            s = 1 - slot % 2
+            s = 1 if slot < PACK else 0
             own = slice(slot * P, (slot + 1) * P)
             nc.tensor.matmul_mx(
                 out=bank,
-                lhsT=value_codes[:, own].bitcast(FP8X4),
+                lhsT=value_codes[slot].bitcast(FP8X4),
                 lhsT_scale=value_scales[:, own],
                 rhs=table_codes[s][:, cols].bitcast(FP8X4),
                 rhs_scale=table_scales[s][:, cols],
-                start=(slot % 2 == 0),
-                stop=(slot % 2 == 1),
+                start=(slot < PACK),
+                stop=(slot >= PACK),
             )
 
-        low = late.tile([P, 2, N], F32, name="low", align_bytes=64, offset=8192 + 2048)
-        high = late.tile([P, 2, N], F32, name="high", align_bytes=64, offset=0)
-        result_rows = late.tile([P, N, PACK], BF16, name="result_rows", align_bytes=64, offset=4096)
+        rest = late.tile([P, LAST, N], F32, name="rest", align_bytes=64, offset=0)
         result_codes = tile("result_codes", [P, N], U32)
         result_scales = tile("result_scales", [P, N], U8)
-        halves = [slice(0, HALF), slice(HALF, N)]
-        whole = slice(0, N)
 
         def result(r, cols):
-            return (low, high)[r // 2][:, r % 2, cols]
+            return first[:, 0, cols] if r == 0 else rest[:, r - 1, cols]
 
         def store_plane(r):
             nc.sync.dma_start(out=plane(out_0, r), in_=result(r, whole))
 
-        sums = []
-
-        def finish(r, rows, bank):
-            sums.append(bank_tile(f"sum{r}", [P, N], bank))
-            quantize_values(rows, 2 * r)
-            for slot in (2 * r, 2 * r + 1):
-                multiply(sums[r][:], slot, whole)
-
-        def copy_out(r):
-            nc.scalar.copy(result(r, whole), sums[r][:])
+        def copy_out(r, copy):
+            copy(result(r, whole), sums[r][:])
             store_plane(r)
 
+        turned01 = turn([pick(0), pick(1)], 0, 4)
+        turned23 = turn([pick(2), pick(3)], 2, 5)
+        turned4 = turn([pick(4)], 4, 6)
+        sums = [bank_tile(f"sum{r}", [P, N], r) for r in range(LAST)]
         rows01 = tile("rows01", [P, 2 * N], BF16)
-        turn([pick(0, False), pick(1, False)], 0, 4, nc.vector.tensor_copy, rows01)
-        picked23 = [pick(2, False), pick(3, False)]
-        picked4 = pick(4, False)
-        rows23 = tile("rows23", [P, 2 * N], BF16, tag="val2_win2")
-        turn(picked23, 2, 5, nc.scalar.copy, rows23)
-        finish(0, rows01, 5)
-        finish(1, rows23, 1)
-        picked5 = pick(5, True)
-        picked6 = pick(6, True)
-        rows45 = late.tile([P, 2 * N], BF16, name="rows45", align_bytes=64, offset=8192)
-        finish(2, turn([picked4, picked5], 4, 6, nc.vector.tensor_copy, rows45), 2)
-        copy_out(0)
-        rows6 = tile("rows6", [P, N], BF16)
-        quantize_values(turn([picked6], 6, 7, nc.scalar.copy, rows6), 6)
-        copy_out(1)
+        rows234 = tile("rows234", [P, 3 * N], BF16)
+        lay_rows(turned01, nc.vector.tensor_copy, rows01[:])
+        lay_rows(turned23, nc.vector.tensor_copy, rows234[:, : 2 * N])
+        quantize_values(rows01, 0, tile("codes01", [P, 2 * P], U32))
+        lay_rows(turned4, nc.vector.tensor_copy, rows234[:, 2 * N :])
         half_sums = [bank_tile(f"half_sum{h}", [P, HALF], 3 + h) for h in range(2)]
+        for r in range(2):
+            multiply(sums[r][:], r, whole)
+        turned5 = turn([pick(5)], 5, 7)
+        quantize_values(rows234, 2, tile("codes234", [P, 3 * P], U32, tag="val_win1"))
+        multiply(sums[0][:], 4, whole)
+        multiply(sums[2][:], 2, whole)
         for h in range(2):
-            multiply(half_sums[h][:], 6, halves[h])
-        picked7 = pick(7, True)
-        copy_out(2)
-        interleave(nc.vector.tensor_copy, result_rows[:, :, 0:2], low[:])
+            multiply(half_sums[h][:], LAST, halves[h])
+        rows5 = tile("rows5", [P, N], BF16)
+        lay_rows(turned5, nc.vector.tensor_copy, rows5[:])
+        turned6 = turn([pick(6)], 6, 5)
+        quantize_values(rows5, 5, late.tile([P, P], U32, name="codes5", align_bytes=64, offset=4 * T + 4 * N))
+        multiply(sums[1][:], 5, whole)
+        first = late.tile([P, 1, N], F32, name="first", align_bytes=64, offset=4 * T)
+        copy_out(0, nc.scalar.copy)
+        picked7 = pick(7, split=True)
+        copy_out(1, nc.scalar.copy)
+        rows6 = late.tile([P, N], BF16, name="rows6", align_bytes=64, offset=LAST * N * 4)
+        lay_rows(turned6, nc.vector.tensor_copy, rows6[:])
+        quantize_values(rows6, 6, tile("codes6", [P, P], U32))
         rows7 = tile("rows7", [P, N], BF16)
-        quantize_values(turn([picked7], 7, 5, nc.scalar.copy, rows7), 7)
+        lay_rows(turn([picked7], 7, 6), nc.scalar.copy, rows7[:])
+        quantize_values(rows7, 7, tile("codes7", [P, P], U32))
+        multiply(sums[2][:], 6, whole)
         for h in range(2):
             multiply(half_sums[h][:], 7, halves[h])
+        result_rows = tile("result_rows", [P, N, PACK], BF16, tag="rows7")
+        nc.vector.tensor_copy(result_rows[:, :, 0], first[:, 0, :])
+        copy_out(2, nc.scalar.copy)
         for h in range(2):
             nc.scalar.copy(result(LAST, halves[h]), half_sums[h][:])
         for h in range(2):
-            interleave(nc.vector.tensor_copy, result_rows[:, halves[h], 2:4], high[:, :, halves[h]])
+            interleave(nc.vector.tensor_copy, result_rows[:, halves[h], 1:], rest[:, :, halves[h]])
         for h in range(2):
             nc.vector.quantize_mx(
                 out=result_codes[:, halves[h]].bitcast(FP8X4),

@@ -81,20 +81,20 @@ def tile_attend_tab_timestable_twostores_pl_kernel(
         def load_key_bytes(q):
             load(key_bytes[32 * q : 32 * q + 4, :].bitcast(I32), keys_scales[0, 4 * q : 4 * q + 4, :].bitcast(I32))
 
-        load(note_win[0][:], plane(notes, 0))
         load(lists[1][:], offs2)
-        load(key_words[:].bitcast(I32), keys_words[0].bitcast(I32))
         load(lists[0][:], offs)
+        load(lists[2][:], offs3)
+        load(note_win[0][:], plane(notes, 0))
+        load(key_words[:].bitcast(I32), keys_words[0].bitcast(I32))
+        load(note_win[1][:], plane(notes, 1))
         for q in range(4):
             load_key_bytes(q)
-        load(note_win[1][:], plane(notes, 1))
         load(note_win[2][:], plane(notes, 2))
         load(note_win[3][:], plane(notes, 3))
-        load(lists[2][:], offs3)
         load(given_win[0][:], plane(given, 0))
+        load(given_win[1][:], plane(given, 1))
         load(factor[0][:], rowf.rearrange("(p t) o -> p (t o)", t=PACK))
         load(factor[1][:], rowf2.rearrange("(p t) o -> p (t o)", t=PACK))
-        load(given_win[1][:], plane(given, 1))
         load(given_win[2][:], plane(given, 2))
         load(given_win[3][:], plane(given, 3))
         load(lists[3][:], offs4)

@@ -81,20 +81,20 @@ def tile_attend_tab_timestable_twostores_pl_kernel(
         def load_key_bytes(q):
             load(key_bytes[32 * q : 32 * q + 4, :].bitcast(I32), keys_scales[0, 4 * q : 4 * q + 4, :].bitcast(I32))
 
-        load(lists[1][:], offs2)
-        load(lists[0][:], offs)
-        load(lists[2][:], offs3)
         load(note_win[0][:], plane(notes, 0))
+        load(lists[1][:], offs2)
         load(key_words[:].bitcast(I32), keys_words[0].bitcast(I32))
-        load(note_win[1][:], plane(notes, 1))
+        load(lists[0][:], offs)
         for q in range(4):
             load_key_bytes(q)
+        load(note_win[1][:], plane(notes, 1))
         load(note_win[2][:], plane(notes, 2))
         load(note_win[3][:], plane(notes, 3))
+        load(lists[2][:], offs3)
         load(given_win[0][:], plane(given, 0))
-        load(given_win[1][:], plane(given, 1))
         load(factor[0][:], rowf.rearrange("(p t) o -> p (t o)", t=PACK))
         load(factor[1][:], rowf2.rearrange("(p t) o -> p (t o)", t=PACK))
+        load(given_win[1][:], plane(given, 1))
         load(given_win[2][:], plane(given, 2))
         load(given_win[3][:], plane(given, 3))
         load(lists[3][:], offs4)
@@ -112,18 +112,22 @@ def tile_attend_tab_timestable_twostores_pl_kernel(
         dealt_words = tile("dealt_words", [P, PACK, P], U16)
         dealt_bytes = tile("dealt_bytes", [P, PACK, P], U8)
         vector_gather(picked_words[:], key_words, lists[0][:])
-        vector_gather(dealt_bytes[:].rearrange("p t m -> p m t"), key_bytes, lists[0][:])
+        picked_bytes = tile("picked_bytes", [P, N], U8)
+        vector_gather(picked_bytes[:], key_bytes, lists[0][:])
         nc.vector.tensor_copy(dealt_words[:], picked_words[:].rearrange("p (m t) -> p t m", t=PACK))
+        nc.vector.tensor_copy(dealt_bytes[:], picked_bytes[:].rearrange("p (m t) -> p t m", t=PACK))
 
         note_rows = tile("note_rows", [P, N, PACK], BF16)
-        interleave(nc.vector.tensor_copy, note_rows[:, :, 0:2], note_planes[:, 0:2, :])
+        nc.vector.tensor_copy(note_rows[:, :, 0:2], note_planes[:, 0:2, :].rearrange("p t j -> p j t"))
         split_gather(note_planes[:, LAST, :], note_win[LAST], lists[1])
         note_codes = tile("note_codes", [P, N], U32)
         note_scales = tile("note_scales", [P, N], U8)
         halves = [slice(0, HALF), slice(HALF, N)]
         whole = slice(0, N)
         for h in (1, 0):
-            interleave(nc.vector.tensor_copy, note_rows[:, halves[h], 2:4], note_planes[:, 2:4, halves[h]])
+            nc.vector.tensor_copy(
+                note_rows[:, halves[h], 2:4], note_planes[:, 2:4, halves[h]].rearrange("p t j -> p j t")
+            )
         for h in (1, 0):
             nc.vector.quantize_mx(
                 out=note_codes[:, halves[h]].bitcast(FP8X4),
@@ -154,19 +158,21 @@ def tile_attend_tab_timestable_twostores_pl_kernel(
         table_rows = [tile(f"table_rows{s}", [P, N, PACK], BF16) for s in range(2)]
         table_codes = [tile(f"table_codes{s}", [P, N], U32) for s in range(2)]
         table_scales = [tile(f"table_scales{s}", [P, N], U8) for s in range(2)]
-        for t in range(PACK):
-            for s in range(2):
-                nc.vector.scalar_tensor_tensor(
-                    out=table_planes[s][:, t, :],
-                    in0=products[t][:],
-                    scalar=factor[s][:, t : t + 1],
-                    in1=given_cols[:, t, :],
-                    op0=MULT,
-                    op1=MULT,
-                )
-        for s in (1, 0):
+
+        def weigh(s, t):
+            nc.vector.scalar_tensor_tensor(
+                out=table_planes[s][:, t, :],
+                in0=products[t][:],
+                scalar=factor[s][:, t : t + 1],
+                in1=given_cols[:, t, :],
+                op0=MULT,
+                op1=MULT,
+            )
+
+        def weave_table(s):
             interleave(nc.vector.tensor_copy, table_rows[s][:], table_planes[s][:])
-        for s in (1, 0):
+
+        def quantize_table(s):
             nc.vector.quantize_mx(
                 out=table_codes[s][:].bitcast(FP8X4),
                 scales=table_scales[s][:],
@@ -238,29 +244,38 @@ def tile_attend_tab_timestable_twostores_pl_kernel(
         turned01 = turn([pick(0), pick(1)], 0, 4)
         turned23 = turn([pick(2), pick(3)], 2, 5)
         turned4 = turn([pick(4)], 4, 6)
+        for s, t in ((1, 0), (0, 0), (1, 1), (0, 1), (1, 2), (1, 3), (0, 2)):
+            weigh(s, t)
+        weave_table(1)
+        weigh(0, 3)
         sums = [bank_tile(f"sum{r}", [P, N], r) for r in range(LAST)]
         rows01 = tile("rows01", [P, 2 * N], BF16)
-        rows234 = tile("rows234", [P, 3 * N], BF16)
         lay_rows(turned01, nc.vector.tensor_copy, rows01[:])
-        lay_rows(turned23, nc.vector.tensor_copy, rows234[:, : 2 * N])
-        quantize_values(rows01, 0, tile("codes01", [P, 2 * P], U32))
-        lay_rows(turned4, nc.vector.tensor_copy, rows234[:, 2 * N :])
-        half_sums = [bank_tile(f"half_sum{h}", [P, HALF], 3 + h) for h in range(2)]
+        quantize_table(1)
+        quantize_values(rows01, 0, tile("codes01", [P, 2 * P], U32, tag="val2_win3"))
         for r in range(2):
             multiply(sums[r][:], r, whole)
-        turned5 = turn([pick(5)], 5, 7)
-        quantize_values(rows234, 2, tile("codes234", [P, 3 * P], U32, tag="val_win1"))
-        multiply(sums[0][:], 4, whole)
+        weave_table(0)
+        rows23 = tile("rows23", [P, 2 * N], BF16, tag="val_win0")
+        lay_rows(turned23, nc.scalar.copy, rows23[:])
+        quantize_table(0)
+        quantize_values(rows23, 2, tile("codes23", [P, 2 * P], U32))
         multiply(sums[2][:], 2, whole)
-        for h in range(2):
-            multiply(half_sums[h][:], LAST, halves[h])
-        rows5 = tile("rows5", [P, N], BF16)
+        turned5 = turn([pick(5)], 5, 7)
+        rows4 = tile("rows4", [P, N], BF16, tag="val_win1")
+        lay_rows(turned4, nc.scalar.copy, rows4[:])
+        quantize_values(rows4, 4, tile("codes4", [P, P], U32))
+        multiply(sums[0][:], 4, whole)
+        turned6 = turn([pick(6, split=True)], 6, 5)
+        rows5 = late.tile([P, N], BF16, name="rows5", align_bytes=64, offset=4 * T + 4 * N)
         lay_rows(turned5, nc.vector.tensor_copy, rows5[:])
-        turned6 = turn([pick(6)], 6, 5)
-        quantize_values(rows5, 5, late.tile([P, P], U32, name="codes5", align_bytes=64, offset=4 * T + 4 * N))
-        multiply(sums[1][:], 5, whole)
+        quantize_values(rows5, 5, tile("codes5", [P, P], U32))
         first = late.tile([P, 1, N], F32, name="first", align_bytes=64, offset=4 * T)
         copy_out(0, nc.scalar.copy)
+        half_sums = [bank_tile(f"half_sum{h}", [P, HALF], bank) for h, bank in enumerate((7, 0))]
+        for h in range(2):
+            multiply(half_sums[h][:], LAST, halves[h])
+        multiply(sums[1][:], 5, whole)
         picked7 = pick(7, split=True)
         copy_out(1, nc.scalar.copy)
         rows6 = late.tile([P, N], BF16, name="rows6", align_bytes=64, offset=LAST * N * 4)

from contextlib import ExitStack

import concourse.mybir as mybir
from concourse.masks import make_identity

D, T, I, J, U, Z, E, Y = 512, 2048, 512, 512, 1024, 1024, 512, 1024
FLOPS = 2 * D * I * J + 2 * 2 * I * E * J

F32 = mybir.dt.float32
BF16 = mybir.dt.bfloat16
I32 = mybir.dt.int32
U32 = mybir.dt.uint32
U16 = mybir.dt.uint16
U8 = mybir.dt.uint8
FP8X4 = mybir.dt.float8_e4m3fn_x4
FP4X4 = mybir.dt.float4_e2m1fn_x4
MULT = mybir.AluOpType.mult
COPY = mybir.ActivationFunctionType.Copy

P = 128
PACK = 4
N = 512
HALF = N // 2
LAST = PACK - 1


def tile_attend_tab_timestable_twostores_pl_kernel(
    tc, keys_words, keys_scales, notes, given, rowf, rowf2, vals, vals2, offs, offs2, offs3, offs4, out_0, out_1, out_2
):
    nc = tc.nc
    with ExitStack() as ctx:
        keep = ctx.enter_context(tc.tile_pool(name="keep", bufs=1))
        late = ctx.enter_context(tc.tile_pool(name="late", bufs=1))
        psum = ctx.enter_context(tc.psum_pool(name="psum", bufs=1))

        def tile(name, shape, dtype, tag=None):
            return keep.tile(shape, dtype, name=name, tag=tag or name, align_bytes=64)

        def bank_tile(name, shape, bank):
            return psum.tile(shape, F32, name=name, tag=f"bank{bank}")

        def plane(src, r):
            return src.rearrange("(p r) c -> p r c", r=PACK)[:, r, :]

        def interleave(engine_copy, dst, src):
            engine_copy(
                dst.rearrange("p (c i) t -> p c t i", i=4),
                src.rearrange("p t (c i) -> p c t i", i=4),
            )

        def scalar_gather(dst, window, offsets):
            nc.scalar.activation(dst, window[:].indirect(offsets), COPY)

        def vector_gather(dst, window, offsets):
            nc.vector.tensor_copy(dst, window[:].indirect(offsets))

        def split_gather(dst, window, offsets):
            cols = HALF // 16
            scalar_gather(dst[:, :HALF], window, offsets[:, :cols])
            vector_gather(dst[:, HALF:], window, offsets[:, cols:])

        lists = [tile(f"list{n}", [P, N // 16], U16) for n in range(4)]
        key_words = tile("key_words", [P, T], U16)
        key_bytes = tile("key_bytes", [P, T], U8)
        note_win = [tile(f"note_win{t}", [P, U], F32) for t in range(PACK)]
        given_win = [tile(f"given_win{t}", [P, Z], F32) for t in range(PACK)]
        val_win = [tile(f"val_win{r}", [P, T], F32) for r in range(2)]
        val_win.append(late.tile([P, T], F32, name="val_win2", align_bytes=64, offset=4 * T))
        val_win.append(late.tile([P, T], F32, name="val_win3", align_bytes=64, offset=0))
        val2_win = [tile(f"val2_win{r}", [P, Y], F32) for r in range(PACK)]
        factor = [tile(f"factor{s}", [P, PACK], F32) for s in range(2)]
        identity = tile("identity", [P, P], F32)

        nc.gpsimd.memset(key_bytes[:, : T // 2].bitcast(I32), 0)
        nc.vector.memset(key_bytes[:, T // 2 :].bitcast(I32), 0)
        make_identity(nc, identity[:])

        def load(dst, src):
            nc.sync.dma_start(out=dst, in_=src)

        def load_key_bytes(q):
            load(key_bytes[32 * q : 32 * q + 4, :].bitcast(I32), keys_scales[0, 4 * q : 4 * q + 4, :].bitcast(I32))

        load(note_win[0][:], plane(notes, 0))
        load(lists[1][:], offs2)
        load(key_words[:].bitcast(I32), keys_words[0].bitcast(I32))
        load(lists[0][:], offs)
        for q in range(4):
            load_key_bytes(q)
        load(note_win[1][:], plane(notes, 1))
        load(note_win[2][:], plane(notes, 2))
        load(note_win[3][:], plane(notes, 3))
        load(lists[2][:], offs3)
        load(given_win[0][:], plane(given, 0))
        load(factor[0][:], rowf.rearrange("(p t) o -> p (t o)", t=PACK))
        load(factor[1][:], rowf2.rearrange("(p t) o -> p (t o)", t=PACK))
        load(given_win[1][:], plane(given, 1))
        load(given_win[2][:], plane(given, 2))
        load(given_win[3][:], plane(given, 3))
        load(lists[3][:], offs4)
        for r in range(PACK):
            load(val2_win[r][:], plane(vals2, r))
        for r in range(PACK):
            load(val_win[r][:], plane(vals, r))

        note_planes = tile("note_planes", [P, PACK, N], BF16)
        scalar_gather(note_planes[:, 0, :], note_win[0], lists[1][:])
        scalar_gather(note_planes[:, 1, :], note_win[1], lists[1][:])
        scalar_gather(note_planes[:, 2, :], note_win[2], lists[1][:])

        picked_words = tile("picked_words", [P, N], U16)
        dealt_words = tile("dealt_words", [P, PACK, P], U16)
        dealt_bytes = tile("dealt_bytes", [P, PACK, P], U8)
        vector_gather(picked_words[:], key_words, lists[0][:])
        picked_bytes = tile("picked_bytes", [P, N], U8)
        vector_gather(picked_bytes[:], key_bytes, lists[0][:])
        nc.vector.tensor_copy(dealt_words[:], picked_words[:].rearrange("p (m t) -> p t m", t=PACK))
        nc.vector.tensor_copy(dealt_bytes[:], picked_bytes[:].rearrange("p (m t) -> p t m", t=PACK))

        note_rows = tile("note_rows", [P, N, PACK], BF16)
        nc.vector.tensor_copy(note_rows[:, :, 0:2], note_planes[:, 0:2, :].rearrange("p t j -> p j t"))
        split_gather(note_planes[:, LAST, :], note_win[LAST], lists[1])
        note_codes = tile("note_codes", [P, N], U32)
        note_scales = tile("note_scales", [P, N], U8)
        halves = [slice(0, HALF), slice(HALF, N)]
        whole = slice(0, N)
        for h in (1, 0):
            nc.vector.tensor_copy(
                note_rows[:, halves[h], 2:4], note_planes[:, 2:4, halves[h]].rearrange("p t j -> p j t")
            )
        for h in (1, 0):
            nc.vector.quantize_mx(
                out=note_codes[:, halves[h]].bitcast(FP8X4),
                scales=note_scales[:, halves[h]],
                in_=note_rows[:, halves[h], :].rearrange("p j t -> p (j t)"),
            )

        given_cols = tile("given_cols", [P, PACK, N], F32)
        for t in range(PACK):
            scalar_gather(given_cols[:, t, :], given_win[t], lists[2][:])

        products = []
        for t in range(PACK):
            bank = bank_tile(f"product{t}", [P, N], t)
            for cols in (halves[::-1] if t == 0 else [whole]):
                nc.tensor.matmul_mx(
                    out=bank[:, cols],
                    lhsT=dealt_words[:, t, :].bitcast(FP4X4),
                    lhsT_scale=dealt_bytes[:, t, :],
                    rhs=note_codes[:, cols].bitcast(FP8X4),
                    rhs_scale=note_scales[:, cols],
                    start=True,
                    stop=True,
                )
            products.append(bank)

        table_planes = [tile(f"table_planes{s}", [P, PACK, N], BF16) for s in range(2)]
        table_rows = [tile(f"table_rows{s}", [P, N, PACK], BF16) for s in range(2)]
        table_codes = [tile(f"table_codes{s}", [P, N], U32) for s in range(2)]
        table_scales = [tile(f"table_scales{s}", [P, N], U8) for s in range(2)]

        def weigh(s, t):
            nc.vector.scalar_tensor_tensor(
                out=table_planes[s][:, t, :],
                in0=products[t][:],
                scalar=factor[s][:, t : t + 1],
                in1=given_cols[:, t, :],
                op0=MULT,
                op1=MULT,
            )

        def weave_table(s):
            interleave(nc.vector.tensor_copy, table_rows[s][:], table_planes[s][:])

        def quantize_table(s):
            nc.vector.quantize_mx(
                out=table_codes[s][:].bitcast(FP8X4),
                scales=table_scales[s][:],
                in_=table_rows[s][:].rearrange("p j t -> p (j t)"),
            )

        value_codes = {}
        value_scales = tile("value_scales", [P, 2 * PACK * P], U8)

        def pick(slot, split=False):
            window, offsets = (val2_win[slot], lists[3]) if slot < PACK else (val_win[slot - PACK], lists[0])
            picked = tile(f"picked{slot}", [P, N], BF16)
            if split:
                split_gather(picked, window, offsets)
            else:
                scalar_gather(picked[:], window, offsets[:])
            return picked

        def turn(picked_tiles, slot, bank):
            turned = bank_tile(f"turned{slot}", [P, len(picked_tiles), 2, P], bank)
            for k, picked in enumerate(picked_tiles):
                pairs = picked[:].bitcast(F32)
                for u in range(2):
                    nc.tensor.transpose(turned[:, k, u, :], pairs[:, u::2], identity[:])
            return turned

        def lay_rows(turned, copy, rows):
            n = turned.shape[1]
            copy(
                rows.bitcast(F32).rearrange("p (k m u) -> p k m u", k=n, u=2),
                turned[:].rearrange("p k u m -> p k m u"),
            )

        def quantize_values(rows, slot, codes):
            n = rows.shape[1] // N
            nc.vector.quantize_mx(
                out=codes[:].bitcast(FP8X4), scales=value_scales[:, slot * P : (slot + n) * P], in_=rows[:]
            )
            for k in range(n):
                value_codes.setdefault(slot + k, codes[:, k * P : (k + 1) * P])

        def multiply(bank, slot, cols):
            s = 1 if slot < PACK else 0
            own = slice(slot * P, (slot + 1) * P)
            nc.tensor.matmul_mx(
                out=bank,
                lhsT=value_codes[slot].bitcast(FP8X4),
                lhsT_scale=value_scales[:, own],
                rhs=table_codes[s][:, cols].bitcast(FP8X4),
                rhs_scale=table_scales[s][:, cols],
                start=(slot < PACK),
                stop=(slot >= PACK),
            )

        rest = late.tile([P, LAST, N], F32, name="rest", align_bytes=64, offset=0)
        result_codes = tile("result_codes", [P, N], U32)
        result_scales = tile("result_scales", [P, N], U8)

        def result(r, cols):
            return first[:, 0, cols] if r == 0 else rest[:, r - 1, cols]

        def store_plane(r):
            nc.sync.dma_start(out=plane(out_0, r), in_=result(r, whole))

        def copy_out(r, copy):
            copy(result(r, whole), sums[r][:])
            store_plane(r)

        turned01 = turn([pick(0), pick(1)], 0, 4)
        turned23 = turn([pick(2), pick(3)], 2, 5)
        turned4 = turn([pick(4)], 4, 6)
        for s, t in ((1, 0), (0, 0), (1, 1), (0, 1), (1, 2), (1, 3), (0, 2)):
            weigh(s, t)
        weave_table(1)
        weigh(0, 3)
        sums = [bank_tile(f"sum{r}", [P, N], r) for r in range(LAST)]
        rows01 = tile("rows01", [P, 2 * N], BF16)
        lay_rows(turned01, nc.vector.tensor_copy, rows01[:])
        quantize_table(1)
        quantize_values(rows01, 0, tile("codes01", [P, 2 * P], U32, tag="val2_win3"))
        for r in range(2):
            multiply(sums[r][:], r, whole)
        weave_table(0)
        rows23 = tile("rows23", [P, 2 * N], BF16, tag="val_win0")
        lay_rows(turned23, nc.scalar.copy, rows23[:])
        quantize_table(0)
        quantize_values(rows23, 2, tile("codes23", [P, 2 * P], U32))
        multiply(sums[2][:], 2, whole)
        turned5 = turn([pick(5)], 5, 7)
        rows4 = tile("rows4", [P, N], BF16, tag="val_win1")
        lay_rows(turned4, nc.scalar.copy, rows4[:])
        quantize_values(rows4, 4, tile("codes4", [P, P], U32))
        multiply(sums[0][:], 4, whole)
        turned6 = turn([pick(6, split=True)], 6, 5)
        rows5 = late.tile([P, N], BF16, name="rows5", align_bytes=64, offset=4 * T + 4 * N)
        lay_rows(turned5, nc.vector.tensor_copy, rows5[:])
        quantize_values(rows5, 5, tile("codes5", [P, P], U32))
        first = late.tile([P, 1, N], F32, name="first", align_bytes=64, offset=4 * T)
        copy_out(0, nc.scalar.copy)
        half_sums = [bank_tile(f"half_sum{h}", [P, HALF], bank) for h, bank in enumerate((7, 0))]
        for h in range(2):
            multiply(half_sums[h][:], LAST, halves[h])
        multiply(sums[1][:], 5, whole)
        picked7 = pick(7, split=True)
        copy_out(1, nc.scalar.copy)
        rows6 = late.tile([P, N], BF16, name="rows6", align_bytes=64, offset=LAST * N * 4)
        lay_rows(turned6, nc.vector.tensor_copy, rows6[:])
        quantize_values(rows6, 6, tile("codes6", [P, P], U32))
        rows7 = tile("rows7", [P, N], BF16)
        lay_rows(turn([picked7], 7, 6), nc.scalar.copy, rows7[:])
        quantize_values(rows7, 7, tile("codes7", [P, P], U32))
        multiply(sums[2][:], 6, whole)
        for h in range(2):
            multiply(half_sums[h][:], 7, halves[h])
        result_rows = tile("result_rows", [P, N, PACK], BF16, tag="rows7")
        nc.vector.tensor_copy(result_rows[:, :, 0], first[:, 0, :])
        copy_out(2, nc.scalar.copy)
        for h in range(2):
            nc.scalar.copy(result(LAST, halves[h]), half_sums[h][:])
        for h in range(2):
            interleave(nc.vector.tensor_copy, result_rows[:, halves[h], 1:], rest[:, :, halves[h]])
        for h in range(2):
            nc.vector.quantize_mx(
                out=result_codes[:, halves[h]].bitcast(FP8X4),
                scales=result_scales[:, halves[h]],
                in_=result_rows[:, halves[h], :].rearrange("p j t -> p (j t)"),
            )
        store_plane(LAST)
        words_out = out_1[0].rearrange("p c r -> p (c r)").bitcast(I32)
        for h in range(2):
            nc.sync.dma_start(out=words_out[:, halves[h]], in_=result_codes[:, halves[h]].bitcast(I32))
        for q in range(4):
            nc.scalar.dma_start(
                out=out_2[0, 4 * q : 4 * q + 4, :].bitcast(I32),
                in_=result_scales[32 * q : 32 * q + 4, :].bitcast(I32),
            )
